import numpy as np
import ml_dtypes


def mxq(x, axis, fmt="e4m3"):
    dtype, down = {"e4m3": (ml_dtypes.float8_e4m3fn, 7), "e5m2": (ml_dtypes.float8_e5m2, 14)}[fmt]
    v = np.moveaxis(np.asarray(x, np.float32).astype(ml_dtypes.bfloat16).astype(np.float64), axis, -1)
    blocks = v.reshape(v.shape[:-1] + (-1, 32))
    amax = np.abs(blocks).max(-1, keepdims=True)
    byte = np.maximum(np.where(amax > 0, np.frexp(amax)[1] - 1 + 127, 0) - down, 1)
    scale = np.exp2(byte - 127.0)
    codes = (blocks / scale).astype(np.float32).astype(dtype).astype(np.float64)
    return np.moveaxis((codes * scale).reshape(v.shape), -1, axis)


WIDE = False


def mx_kscale(k):
    if not WIDE:
        return np.ones(k)
    levels = np.array([10, -10, 5, -5, 0])
    if k % 512:
        return np.exp2(np.random.permutation(np.resize(levels, k // 32))).repeat(32)
    a = np.empty((k // 512, 16))
    for p in range(k // 512):
        a[p, :8] = np.random.permutation(np.resize(levels, 8))
        for g in range(8):
            far = levels[np.abs(levels - a[p, g]) >= 10]
            a[p, g + 8] = far[np.random.randint(len(far))]
    return np.exp2(a.ravel()).repeat(32)


def f64(x):
    return np.asarray(x).astype(np.float64)


def striped(idx):
    return np.tile(np.asarray(idx).reshape(-1, 16).T, (8, 1)).astype(np.uint16)


def unstriped(offs):
    return offs[:16].T.reshape(-1).astype(np.int64)


E2M1 = np.array([0.0, 0.5, 1.0, 1.5, 2.0, 3.0, 4.0, 6.0, -0.0, -0.5, -1.0, -1.5, -2.0, -3.0, -4.0, -6.0])


def pack_weight(w, fmt):
    k, n = w.shape
    w = f64(np.asarray(w, np.float32).astype(ml_dtypes.bfloat16)).reshape(k // 32, 32, n)
    amax = np.abs(w).max(1)
    if fmt == "e4m3":
        byte = np.frexp(amax)[1] - 1 + 127 - 7
    else:
        mant, ex = np.frexp(amax / 6.0)
        byte = np.where(mant > 0.5, ex, ex - 1) + 127
    byte = np.clip(np.where(amax > 0, byte, 1), 1, 254)
    scaled = (w * np.exp2(127.0 - byte)[:, None, :]).reshape(k, n).astype(np.float32)
    by_word = np.ascontiguousarray(scaled.reshape(k // 512, 128, 4, n).transpose(0, 1, 3, 2))
    if fmt == "e4m3":
        words = by_word.astype(ml_dtypes.float8_e4m3fn).view(np.uint8)
    else:
        c = by_word.astype(ml_dtypes.float4_e2m1fn).view(np.uint8) & 0xF
        words = (c[..., 0::2] | (c[..., 1::2] << 4)).reshape(k // 512, 128, 2 * n)
    return np.ascontiguousarray(words), np.ascontiguousarray(byte.astype(np.uint8).reshape(k // 512, 16, n))


def unpack_weight(words, scales, fmt):
    g, _, n = scales.shape
    words = np.ascontiguousarray(words).reshape(g, 128, n, -1)
    if fmt == "e4m3":
        vals = words.view(ml_dtypes.float8_e4m3fn).astype(np.float64)
    else:
        nib = np.empty((g, 128, n, 4), np.uint8)
        nib[..., 0::2] = words & 0xF
        nib[..., 1::2] = words >> 4
        vals = E2M1[nib]
    vals = vals * np.repeat(np.exp2(scales.astype(np.float64) - 127.0), 8, axis=1)[..., None]
    return vals.transpose(0, 1, 3, 2).reshape(g * 512, n)


B, N, T, D, DV, NQ = 1, 1024, 4096, 1024, 256, 256
PAGE = 512
CAP = 2.0


def setup_inputs():
    n = np.random.standard_normal
    pages = np.random.permutation(T // PAGE)[:B * N // PAGE]
    idx = (pages[:, None] * PAGE + np.arange(PAGE)[None, :]).reshape(-1)
    s = mx_kscale(D)[:, None]
    u = np.ones(T)
    u[idx] = mx_kscale(B * N)
    r = np.random.uniform(0.5, 2.0, T)
    k = n((D, T)) / s
    v = n((DV, T)) / (u * r)
    kp = pack_weight(k, "e2m1")
    vp = pack_weight(v.T, "e4m3")
    return {
        "qT": (n((B, D, NQ)) * s * (1.00 / np.sqrt(D))).astype(np.float32),
        "k_words": np.ascontiguousarray(kp[0].reshape(D // 1024, 2, 128, T, 2).transpose(0, 2, 3, 1, 4)).reshape(D // 1024, 128, T, 4),
        "k_scales": kp[1],
        "v_words": vp[0],
        "v_scales": vp[1],
        "vs": np.tile(u * r, (128, 1)).astype(np.float32),
        "kb": np.tile(n(T), (128, 1)).astype(np.float32),
        "offs": striped(idx),
        "voffs": striped((pages[:, None] * DV + np.arange(DV)[None, :]).reshape(-1)),
    }


def reference(qT, k_words, k_scales, v_words, v_scales, vs, kb, offs, voffs):
    idx = unstriped(offs)
    k = unpack_weight(k_words.reshape(D // 1024, 128, T, 2, 2).transpose(0, 3, 1, 2, 4).reshape(D // 512, 128, 2 * T), k_scales, "e2m1")
    v = unpack_weight(v_words, v_scales, "e4m3")
    v = v.reshape(T // 512, 512, DV)[unstriped(voffs)[::DV] // DV].reshape(B, N, DV)
    pick = lambda x: x[:, idx].reshape(x.shape[0], B, N).transpose(1, 0, 2)
    q = f64(qT)
    score = mxq(q, 1, "e4m3").transpose(0, 2, 1) @ pick(k)
    score = score + pick(f64(kb))[:, :1, :]
    score = CAP * np.tanh(score / CAP)
    p = 1.0 / (1.0 + np.exp(-score))
    w = p * pick(f64(vs))[:, :1, :]
    y = mxq(w, 2, "e4m3") @ v
    y = y / 16.0
    return y

@@ -1,0 +1,202 @@
+from contextlib import ExitStack
+
+import concourse.mybir as mybir
+from concourse.masks import make_identity
+
+F32 = mybir.dt.float32
+BF16 = mybir.dt.bfloat16
+I32 = mybir.dt.int32
+U32 = mybir.dt.uint32
+U16 = mybir.dt.uint16
+U8 = mybir.dt.uint8
+FP8X4 = mybir.dt.float8_e4m3fn_x4
+FP4X4 = mybir.dt.float4_e2m1fn_x4
+ACT = mybir.ActivationFunctionType
+ALU = mybir.AluOpType
+
+P = 128
+PACK = 4
+T, D, DV, NQ, N = 4096, 1024, 256, 256, 1024
+PAGE = 512
+PAGES = N // PAGE
+POOL_PAGES = T // PAGE
+PASSES = D // 512
+HALVES = NQ // P
+
+FLOPS = 2 * NQ * N * D + 2 * NQ * N * DV
+BYTES = 4 * D * NQ + P * T * 4 + 32 * T + POOL_PAGES * P * DV * 4 + POOL_PAGES * 16 * DV + 2 * 4 * T + 2 * P * 96 + 4 * NQ * DV
+
+
+def tile_attend_pkv4_sigm_cap_kb_kernel(tc, qT, k_words, k_scales, v_words, v_scales, vs, kb, offs, voffs, out):
+    nc = tc.nc
+    with ExitStack() as ctx:
+        sb = ctx.enter_context(tc.tile_pool(name="sb", bufs=1))
+        ps = ctx.enter_context(tc.psum_pool(name="ps", bufs=1))
+
+        def tile(name, shape, dtype):
+            return sb.tile(shape, dtype, name=name, align_bytes=64)
+
+        key_list = sb.tile([P, N // 16], U16, name="key_list")
+        nc.sync.dma_start(key_list[:], offs)
+
+        ks_pool = tile("ks_pool", [P, T], U8)
+        nc.vector.memset(ks_pool[0:96, :].bitcast(I32), 0)
+        nc.sync.dma_start(ks_pool[96:128, :].bitcast(I32), k_scales.bitcast(I32).rearrange("o f c -> f o c"))
+
+        kb_pool = tile("kb_pool", [P, T], F32)
+        nc.vector.memset(kb_pool[0:127, :], 0.0)
+        nc.sync.dma_start(kb_pool[127:128, :], kb[0:1, :])
+
+        q_raw = [tile("q_raw%d" % o, [P, PACK, NQ], F32) for o in range(PASSES)]
+        q_rows = qT[0].rearrange("(o p j) q -> o p j q", o=PASSES, j=PACK)
+        for o in range(PASSES):
+            nc.sync.dma_start(q_raw[o][:], q_rows[o])
+        kw_pool = tile("kw_pool", [P, T], I32)
+        nc.sync.dma_start(kw_pool[:], k_words[0].rearrange("p t b -> p (t b)").bitcast(I32))
+
+        value_list = sb.tile([P, PAGES * DV // 16], U16, name="value_list")
+        nc.sync.dma_start(value_list[:], voffs)
+        vs_pool = tile("vs_pool", [P, T], F32)
+        nc.sync.dma_start(vs_pool[:], vs)
+        vw_pool = tile("vw_pool", [P, POOL_PAGES * DV], I32)
+        nc.sync.dma_start(
+            vw_pool[:].rearrange("p (u e) -> p u e", u=POOL_PAGES),
+            v_words.rearrange("u p e b -> p u (e b)").bitcast(I32),
+        )
+
+        ident = tile("ident", [P, P], F32)
+        make_identity(nc, ident[:])
+        k_plane = tile("k_plane", [P, PASSES * N], U8)
+        nc.gpsimd.memset(k_plane[:].bitcast(I32), 0)
+        vsc_pool = tile("vsc_pool", [P, POOL_PAGES * DV], U8)
+        nc.gpsimd.memset(vsc_pool[:].bitcast(I32), 0)
+        for quad in range(4):
+            nc.gpsimd.dma_start(
+                vsc_pool[32 * quad : 32 * quad + 4, :].bitcast(I32).rearrange("p (u e) -> p u e", u=POOL_PAGES),
+                v_scales[:, 4 * quad : 4 * quad + 4, :].bitcast(I32).rearrange("u f e -> f u e"),
+            )
+
+        ks_listed = tile("ks_listed", [P, N], U8)
+        nc.vector.tensor_copy(ks_listed[:], ks_pool[:].indirect(key_list[:]))
+        ks_dealt = tile("ks_dealt", [P, N], U8)
+        nc.vector.tensor_copy(
+            ks_dealt[:].rearrange("p (g t s) -> p g t s", g=PAGES, t=PACK),
+            ks_listed[:].rearrange("p (g s t) -> p g t s", g=PAGES, t=PACK),
+        )
+        for quad in range(4):
+            nc.scalar.dma_start(
+                k_plane[32 * quad : 32 * quad + 4, :].bitcast(I32).rearrange("p (o c) -> p o c", o=PASSES),
+                ks_dealt[96 + 8 * quad : 96 + 8 * quad + 8, :].bitcast(I32),
+            )
+
+        def listed_columns(name, pool_tile, bank_tags):
+            halved = []
+            for g in range(PAGES):
+                listed = tile("%s_listed%d" % (name, g), [P, PAGE], F32)
+                nc.vector.tensor_copy(listed[:], pool_tile[:].indirect(key_list[:, 32 * g : 32 * (g + 1)]))
+                turned = ps.tile([P, PACK, P], F32, name="%s_turned%d" % (name, g), tag=bank_tags[g])
+                for t in range(PACK):
+                    nc.tensor.transpose(turned[:, t, :], listed[:, t::PACK], ident[:])
+                column = tile("%s_halved%d" % (name, g), [P, PACK], F32)
+                nc.scalar.activation(column[:], turned[:, :, P - 1], ACT.Copy, scale=0.5)
+                halved.append(column)
+            return halved
+
+        half_kb = listed_columns("kb", kb_pool, ["kb_bank0", "kb_bank1"])
+
+        q_codes, q_scales, q_woven = [], [], []
+        for o in range(PASSES):
+            woven = tile("q_woven%d" % o, [P, NQ * PACK], BF16)
+            nc.scalar.copy(
+                woven[:].rearrange("p (c i j) -> p c j i", i=4, j=PACK),
+                q_raw[o][:].rearrange("p j (c i) -> p c j i", i=4),
+            )
+            q_woven.append(woven)
+
+        def key_words(g):
+            listed = tile("kw_listed%d" % g, [P, PAGE], U32)
+            nc.vector.tensor_copy(listed[:], kw_pool[:].bitcast(U32).indirect(key_list[:, 32 * g : 32 * (g + 1)]))
+            dealt = tile("kw_dealt%d" % g, [P, PASSES * PAGE * 2], U8)
+            nc.vector.tensor_copy(
+                dealt[:].bitcast(U16).rearrange("p (o t c i) -> p o c t i", o=PASSES, t=PACK, i=4),
+                listed[:].bitcast(U16).rearrange("p (c i t o) -> p o c t i", o=PASSES, t=PACK, i=4),
+            )
+            return dealt
+
+        kw_dealt = [key_words(0)]
+        for o in range(PASSES):
+            codes = tile("q_codes%d" % o, [P, NQ], U32)
+            scales = tile("q_scales%d" % o, [P, NQ], U8)
+            nc.vector.quantize_mx(out=codes[:].bitcast(FP8X4), scales=scales[:], in_=q_woven[o][:])
+            q_codes.append(codes)
+            q_scales.append(scales)
+        kw_dealt.append(key_words(1))
+
+        inner = [tile("inner%d" % g, [P, PACK, NQ], F32) for g in range(PAGES)]
+        outer = {}
+        for g in range(PAGES):
+            for pair in range(PACK // 2):
+                bank = ps.tile([P, 2, NQ], F32, name="scores%d_%d" % (g, pair), tag="scores%d_%d" % (g, pair))
+                for u in range(2):
+                    t = 2 * pair + u
+                    for h in range(HALVES):
+                        for o in range(PASSES):
+                            kcol = (o * PACK + t) * P
+                            scol = o * N + g * PAGE + t * P
+                            nc.tensor.matmul_mx(
+                                out=bank[:, u, h * P : (h + 1) * P],
+                                lhsT=kw_dealt[g][:, 2 * kcol : 2 * (kcol + P)].bitcast(FP4X4),
+                                lhsT_scale=k_plane[:, scol : scol + P],
+                                rhs=q_codes[o][:, h * P : (h + 1) * P].bitcast(FP8X4),
+                                rhs_scale=q_scales[o][:, h * P : (h + 1) * P],
+                                start=(o == 0),
+                                stop=(o == PASSES - 1),
+                            )
+                for u in range(2):
+                    t = 2 * pair + u
+                    nc.scalar.activation(inner[g][:, t, :], bank[:, u, :], ACT.Tanh, bias=half_kb[g][:, t : t + 1], scale=0.5)
+            for h in range(HALVES):
+                woven = tile("outer%d_%d" % (g, h), [P, P * PACK], F32)
+                nc.scalar.activation(
+                    woven[:].rearrange("p (c i t) -> p c t i", i=4, t=PACK),
+                    inner[g][:, :, h * P : (h + 1) * P].rearrange("p t (c i) -> p c t i", i=4),
+                    ACT.Tanh,
+                )
+                outer[g, h] = woven
+
+        vsc_listed = tile("vsc_listed", [P, PAGES * DV], U8)
+        nc.vector.tensor_copy(vsc_listed[:], vsc_pool[:].indirect(value_list[:]))
+        half_vs = listed_columns("vs", vs_pool, ["scores0_0", "scores0_1"])
+        vw_listed = tile("vw_listed", [P, PAGES * DV], U32)
+        nc.vector.tensor_copy(vw_listed[:], vw_pool[:].bitcast(U32).indirect(value_list[:]))
+
+        w_bf = {}
+        for h in range(HALVES):
+            for g in range(PAGES):
+                w = tile("w%d_%d" % (g, h), [P, P * PACK], BF16)
+                nc.vector.scalar_tensor_tensor(
+                    out=w[:].rearrange("p (q t) -> p q t", t=PACK),
+                    in0=outer[g, h][:].rearrange("p (q t) -> p q t", t=PACK),
+                    scalar=1.0,
+                    in1=half_vs[g][:].unsqueeze(1).to_broadcast([P, P, PACK]),
+                    op0=ALU.add,
+                    op1=ALU.mult,
+                )
+                w_bf[g, h] = w
+            acc = ps.tile([P, DV], F32, name="acc%d" % h)
+            for g in range(PAGES):
+                codes = tile("w_codes%d_%d" % (g, h), [P, P], U32)
+                scales = tile("w_scales%d_%d" % (g, h), [P, P], U8)
+                nc.vector.quantize_mx(out=codes[:].bitcast(FP8X4), scales=scales[:], in_=w_bf[g, h][:])
+                nc.tensor.matmul_mx(
+                    out=acc[:],
+                    lhsT=codes[:].bitcast(FP8X4),
+                    lhsT_scale=scales[:],
+                    rhs=vw_listed[:, g * DV : (g + 1) * DV].bitcast(FP8X4),
+                    rhs_scale=vsc_listed[:, g * DV : (g + 1) * DV],
+                    start=(g == 0),
+                    stop=(g == PAGES - 1),
+                )
+            result = tile("result%d" % h, [P, DV], F32)
+            nc.scalar.activation(result[:], acc[:], ACT.Copy, scale=1.0 / 16.0)
+            nc.sync.dma_start(out[0, h * P : (h + 1) * P, :], result[:])

@@ -22,6 +22,7 @@ PAGES = N // PAGE
 POOL_PAGES = T // PAGE
 PASSES = D // 512
 HALVES = NQ // P
+CLEAR = 512
 
 FLOPS = 2 * NQ * N * D + 2 * NQ * N * DV
 BYTES = 4 * D * NQ + P * T * 4 + 32 * T + POOL_PAGES * P * DV * 4 + POOL_PAGES * 16 * DV + 2 * 4 * T + 2 * P * 96 + 4 * NQ * DV
@@ -33,19 +34,34 @@ def tile_attend_pkv4_sigm_cap_kb_kernel(tc, qT, k_words, k_scales, v_words, v_sc
         sb = ctx.enter_context(tc.tile_pool(name="sb", bufs=1))
         ps = ctx.enter_context(tc.psum_pool(name="ps", bufs=1))
 
-        def tile(name, shape, dtype):
-            return sb.tile(shape, dtype, name=name, align_bytes=64)
+        def tile(name, shape, dtype, tag=None):
+            return sb.tile(shape, dtype, name=name, tag=tag or name, align_bytes=64)
+
+        def clear_odd(words):
+            cut = words.shape[1] // 2 + 1
+            nc.vector.memset(words[:, :cut], 0)
+            nc.vector.memset(words[:, cut:], 0)
+
+        def one_row_pool(name, source):
+            pool_tile = tile(name, [P, T], F32)
+            for c in range(0, T, CLEAR):
+                nc.gpsimd.memset(pool_tile[0 : P - 1, c : c + CLEAR], 0.0)
+            nc.sync.dma_start(pool_tile[P - 1 : P, :], source[0:1, :])
+            return pool_tile
+
+        warm_in = tile("warm_in", [P, 1], F32)
+        warm_out = tile("warm_out", [P, 1], F32)
+        nc.vector.memset(warm_in[:], 0.0)
+        nc.scalar.activation(warm_out[:], warm_in[:], ACT.Tanh)
 
         key_list = sb.tile([P, N // 16], U16, name="key_list")
         nc.sync.dma_start(key_list[:], offs)
 
         ks_pool = tile("ks_pool", [P, T], U8)
-        nc.vector.memset(ks_pool[0:96, :].bitcast(I32), 0)
+        clear_odd(ks_pool[0:96, :].bitcast(I32))
         nc.sync.dma_start(ks_pool[96:128, :].bitcast(I32), k_scales.bitcast(I32).rearrange("o f c -> f o c"))
 
-        kb_pool = tile("kb_pool", [P, T], F32)
-        nc.vector.memset(kb_pool[0:127, :], 0.0)
-        nc.sync.dma_start(kb_pool[127:128, :], kb[0:1, :])
+        kb_pool = one_row_pool("kb_pool", kb)
 
         q_raw = [tile("q_raw%d" % o, [P, PACK, NQ], F32) for o in range(PASSES)]
         q_rows = qT[0].rearrange("(o p j) q -> o p j q", o=PASSES, j=PACK)
@@ -56,53 +72,10 @@ def tile_attend_pkv4_sigm_cap_kb_kernel(tc, qT, k_words, k_scales, v_words, v_sc
 
         value_list = sb.tile([P, PAGES * DV // 16], U16, name="value_list")
         nc.sync.dma_start(value_list[:], voffs)
-        vs_pool = tile("vs_pool", [P, T], F32)
-        nc.sync.dma_start(vs_pool[:], vs)
-        vw_pool = tile("vw_pool", [P, POOL_PAGES * DV], I32)
-        nc.sync.dma_start(
-            vw_pool[:].rearrange("p (u e) -> p u e", u=POOL_PAGES),
-            v_words.rearrange("u p e b -> p u (e b)").bitcast(I32),
-        )
-
         ident = tile("ident", [P, P], F32)
         make_identity(nc, ident[:])
         k_plane = tile("k_plane", [P, PASSES * N], U8)
-        nc.gpsimd.memset(k_plane[:].bitcast(I32), 0)
-        vsc_pool = tile("vsc_pool", [P, POOL_PAGES * DV], U8)
-        nc.gpsimd.memset(vsc_pool[:].bitcast(I32), 0)
-        for quad in range(4):
-            nc.gpsimd.dma_start(
-                vsc_pool[32 * quad : 32 * quad + 4, :].bitcast(I32).rearrange("p (u e) -> p u e", u=POOL_PAGES),
-                v_scales[:, 4 * quad : 4 * quad + 4, :].bitcast(I32).rearrange("u f e -> f u e"),
-            )
-
-        ks_listed = tile("ks_listed", [P, N], U8)
-        nc.vector.tensor_copy(ks_listed[:], ks_pool[:].indirect(key_list[:]))
-        ks_dealt = tile("ks_dealt", [P, N], U8)
-        nc.vector.tensor_copy(
-            ks_dealt[:].rearrange("p (g t s) -> p g t s", g=PAGES, t=PACK),
-            ks_listed[:].rearrange("p (g s t) -> p g t s", g=PAGES, t=PACK),
-        )
-        for quad in range(4):
-            nc.scalar.dma_start(
-                k_plane[32 * quad : 32 * quad + 4, :].bitcast(I32).rearrange("p (o c) -> p o c", o=PASSES),
-                ks_dealt[96 + 8 * quad : 96 + 8 * quad + 8, :].bitcast(I32),
-            )
-
-        def listed_columns(name, pool_tile, bank_tags):
-            halved = []
-            for g in range(PAGES):
-                listed = tile("%s_listed%d" % (name, g), [P, PAGE], F32)
-                nc.vector.tensor_copy(listed[:], pool_tile[:].indirect(key_list[:, 32 * g : 32 * (g + 1)]))
-                turned = ps.tile([P, PACK, P], F32, name="%s_turned%d" % (name, g), tag=bank_tags[g])
-                for t in range(PACK):
-                    nc.tensor.transpose(turned[:, t, :], listed[:, t::PACK], ident[:])
-                column = tile("%s_halved%d" % (name, g), [P, PACK], F32)
-                nc.scalar.activation(column[:], turned[:, :, P - 1], ACT.Copy, scale=0.5)
-                halved.append(column)
-            return halved
-
-        half_kb = listed_columns("kb", kb_pool, ["kb_bank0", "kb_bank1"])
+        clear_odd(k_plane[:].bitcast(I32))
 
         q_codes, q_scales, q_woven = [], [], []
         for o in range(PASSES):
@@ -113,8 +86,54 @@ def tile_attend_pkv4_sigm_cap_kb_kernel(tc, qT, k_words, k_scales, v_words, v_sc
             )
             q_woven.append(woven)
 
+        ks_listed = tile("ks_listed", [P, N], U8)
+        nc.vector.tensor_copy(ks_listed[:], ks_pool[:].indirect(key_list[:]))
+        ks_dealt = tile("ks_dealt", [P, N], U8, tag="q_raw0")
+        nc.vector.tensor_copy(
+            ks_dealt[:].rearrange("p (g t s) -> p g t s", g=PAGES, t=PACK),
+            ks_listed[:].rearrange("p (g s t) -> p g t s", g=PAGES, t=PACK),
+        )
+        for quad in range(4):
+            nc.scalar.dma_start(
+                k_plane[32 * quad : 32 * quad + 4, :].bitcast(I32).rearrange("p (o c) -> p o c", o=PASSES),
+                ks_dealt[96 + 8 * quad : 96 + 8 * quad + 8, :].bitcast(I32),
+            )
+
+        def turned_columns(name, pool_tile, listed_tag, bank_tags):
+            banks = []
+            both = tile(name + "_listed", [P, N], F32, tag=listed_tag)
+            for g in range(PAGES):
+                listed = both[:, PAGE * g : PAGE * (g + 1)]
+                nc.vector.tensor_copy(listed, pool_tile[:].indirect(key_list[:, 32 * g : 32 * (g + 1)]))
+                turned = ps.tile([P, PACK, P], F32, name="%s_turned%d" % (name, g), tag=bank_tags[g])
+                for t in range(PACK):
+                    nc.tensor.transpose(turned[:, t, :], listed[:, t::PACK], ident[:])
+                banks.append(turned)
+            return banks
+
+        half_kb = []
+        for g, turned in enumerate(turned_columns("kb", kb_pool, "kb_listed", ["kb_bank0", "kb_bank1"])):
+            column = tile("half_kb%d" % g, [P, PACK], F32)
+            nc.scalar.activation(column[:], turned[:, :, P - 1], ACT.Copy, scale=0.5)
+            half_kb.append(column)
+
+        vw_pool = tile("vw_pool", [P, POOL_PAGES * DV], I32, tag="q_raw0")
+        nc.sync.dma_start(
+            vw_pool[:].rearrange("p (u e) -> p u e", u=POOL_PAGES),
+            v_words.rearrange("u p e b -> p u (e b)").bitcast(I32),
+        )
+        vsc_pool = tile("vsc_pool", [P, POOL_PAGES * DV], U8, tag="kb_listed")
+        nc.gpsimd.memset(vsc_pool[:].bitcast(I32), 0)
+        for quad in range(4):
+            nc.sync.dma_start(
+                vsc_pool[32 * quad : 32 * quad + 4, :].bitcast(I32).rearrange("p (u e) -> p u e", u=POOL_PAGES),
+                v_scales[:, 4 * quad : 4 * quad + 4, :].bitcast(I32).rearrange("u f e -> f u e"),
+            )
+
+        vs_pool = one_row_pool("vs_pool", vs)
+
         def key_words(g):
-            listed = tile("kw_listed%d" % g, [P, PAGE], U32)
+            listed = tile("kw_listed%d" % g, [P, PAGE], U32, tag=["kw_listed0", "q_woven1"][g])
             nc.vector.tensor_copy(listed[:], kw_pool[:].bitcast(U32).indirect(key_list[:, 32 * g : 32 * (g + 1)]))
             dealt = tile("kw_dealt%d" % g, [P, PASSES * PAGE * 2], U8)
             nc.vector.tensor_copy(
@@ -164,11 +183,14 @@ def tile_attend_pkv4_sigm_cap_kb_kernel(tc, qT, k_words, k_scales, v_words, v_sc
                 )
                 outer[g, h] = woven
 
+        vs_banks = turned_columns("vs", vs_pool, "q_woven1", ["scores0_0", "scores0_1"])
         vsc_listed = tile("vsc_listed", [P, PAGES * DV], U8)
         nc.vector.tensor_copy(vsc_listed[:], vsc_pool[:].indirect(value_list[:]))
-        half_vs = listed_columns("vs", vs_pool, ["scores0_0", "scores0_1"])
-        vw_listed = tile("vw_listed", [P, PAGES * DV], U32)
+        vw_listed = tile("vw_listed", [P, PAGES * DV], U32, tag="kb_listed")
         nc.vector.tensor_copy(vw_listed[:], vw_pool[:].bitcast(U32).indirect(value_list[:]))
+        half_vs = tile("half_vs", [P, PAGES * PACK], F32, tag="q_raw0")
+        for g in range(PAGES):
+            nc.vector.tensor_scalar_mul(half_vs[:, PACK * g : PACK * (g + 1)], vs_banks[g][:, :, P - 1], 0.5)
 
         w_bf = {}
         for h in range(HALVES):
@@ -178,7 +200,7 @@ def tile_attend_pkv4_sigm_cap_kb_kernel(tc, qT, k_words, k_scales, v_words, v_sc
                     out=w[:].rearrange("p (q t) -> p q t", t=PACK),
                     in0=outer[g, h][:].rearrange("p (q t) -> p q t", t=PACK),
                     scalar=1.0,
-                    in1=half_vs[g][:].unsqueeze(1).to_broadcast([P, P, PACK]),
+                    in1=half_vs[:, PACK * g : PACK * (g + 1)].unsqueeze(1).to_broadcast([P, P, PACK]),
                     op0=ALU.add,
                     op1=ALU.mult,
                 )

from contextlib import ExitStack

import concourse.mybir as mybir
from concourse.masks import make_identity

F32 = mybir.dt.float32
BF16 = mybir.dt.bfloat16
I32 = mybir.dt.int32
U32 = mybir.dt.uint32
U16 = mybir.dt.uint16
U8 = mybir.dt.uint8
FP8X4 = mybir.dt.float8_e4m3fn_x4
FP4X4 = mybir.dt.float4_e2m1fn_x4
ACT = mybir.ActivationFunctionType
ALU = mybir.AluOpType

P = 128
PACK = 4
T, D, DV, NQ, N = 4096, 1024, 256, 256, 1024
PAGE = 512
PAGES = N // PAGE
POOL_PAGES = T // PAGE
PASSES = D // 512
HALVES = NQ // P
CLEAR = 512

FLOPS = 2 * NQ * N * D + 2 * NQ * N * DV
BYTES = 4 * D * NQ + P * T * 4 + 32 * T + POOL_PAGES * P * DV * 4 + POOL_PAGES * 16 * DV + 2 * 4 * T + 2 * P * 96 + 4 * NQ * DV


def tile_attend_pkv4_sigm_cap_kb_kernel(tc, qT, k_words, k_scales, v_words, v_scales, vs, kb, offs, voffs, out):
    nc = tc.nc
    with ExitStack() as ctx:
        sb = ctx.enter_context(tc.tile_pool(name="sb", bufs=1))
        ps = ctx.enter_context(tc.psum_pool(name="ps", bufs=1))

        def tile(name, shape, dtype, tag=None):
            return sb.tile(shape, dtype, name=name, tag=tag or name, align_bytes=64)

        def clear_odd(words):
            cut = words.shape[1] // 2 + 1
            nc.vector.memset(words[:, :cut], 0)
            nc.vector.memset(words[:, cut:], 0)

        def one_row_pool(name, source):
            pool_tile = tile(name, [P, T], F32)
            for c in range(0, T, CLEAR):
                nc.gpsimd.memset(pool_tile[0 : P - 1, c : c + CLEAR], 0.0)
            nc.sync.dma_start(pool_tile[P - 1 : P, :], source[0:1, :])
            return pool_tile

        warm_in = tile("warm_in", [P, 1], F32)
        warm_out = tile("warm_out", [P, 1], F32)
        nc.vector.memset(warm_in[:], 0.0)
        nc.scalar.activation(warm_out[:], warm_in[:], ACT.Tanh)

        key_list = sb.tile([P, N // 16], U16, name="key_list")
        nc.sync.dma_start(key_list[:], offs)

        ks_pool = tile("ks_pool", [P, T], U8)
        clear_odd(ks_pool[0:96, :].bitcast(I32))
        nc.sync.dma_start(ks_pool[96:128, :].bitcast(I32), k_scales.bitcast(I32).rearrange("o f c -> f o c"))

        kb_pool = one_row_pool("kb_pool", kb)

        q_raw = [tile("q_raw%d" % o, [P, PACK, NQ], F32) for o in range(PASSES)]
        q_rows = qT[0].rearrange("(o p j) q -> o p j q", o=PASSES, j=PACK)
        for o in range(PASSES):
            nc.sync.dma_start(q_raw[o][:], q_rows[o])
        kw_pool = tile("kw_pool", [P, T], I32)
        nc.sync.dma_start(kw_pool[:], k_words[0].rearrange("p t b -> p (t b)").bitcast(I32))

        value_list = sb.tile([P, PAGES * DV // 16], U16, name="value_list")
        nc.sync.dma_start(value_list[:], voffs)
        ident = tile("ident", [P, P], F32)
        make_identity(nc, ident[:])
        k_plane = tile("k_plane", [P, PASSES * N], U8)
        clear_odd(k_plane[:].bitcast(I32))

        q_codes, q_scales, q_woven = [], [], []
        for o in range(PASSES):
            woven = tile("q_woven%d" % o, [P, NQ * PACK], BF16)
            nc.scalar.copy(
                woven[:].rearrange("p (c i j) -> p c j i", i=4, j=PACK),
                q_raw[o][:].rearrange("p j (c i) -> p c j i", i=4),
            )
            q_woven.append(woven)

        ks_listed = tile("ks_listed", [P, N], U8)
        nc.vector.tensor_copy(ks_listed[:], ks_pool[:].indirect(key_list[:]))
        ks_dealt = tile("ks_dealt", [P, N], U8, tag="q_raw0")
        nc.vector.tensor_copy(
            ks_dealt[:].rearrange("p (g t s) -> p g t s", g=PAGES, t=PACK),
            ks_listed[:].rearrange("p (g s t) -> p g t s", g=PAGES, t=PACK),
        )
        for quad in range(4):
            nc.scalar.dma_start(
                k_plane[32 * quad : 32 * quad + 4, :].bitcast(I32).rearrange("p (o c) -> p o c", o=PASSES),
                ks_dealt[96 + 8 * quad : 96 + 8 * quad + 8, :].bitcast(I32),
            )

        def turned_columns(name, pool_tile, listed_tag, bank_tags):
            banks = []
            both = tile(name + "_listed", [P, N], F32, tag=listed_tag)
            for g in range(PAGES):
                listed = both[:, PAGE * g : PAGE * (g + 1)]
                nc.vector.tensor_copy(listed, pool_tile[:].indirect(key_list[:, 32 * g : 32 * (g + 1)]))
                turned = ps.tile([P, PACK, P], F32, name="%s_turned%d" % (name, g), tag=bank_tags[g])
                for t in range(PACK):
                    nc.tensor.transpose(turned[:, t, :], listed[:, t::PACK], ident[:])
                banks.append(turned)
            return banks

        half_kb = []
        for g, turned in enumerate(turned_columns("kb", kb_pool, "kb_listed", ["kb_bank0", "kb_bank1"])):
            column = tile("half_kb%d" % g, [P, PACK], F32)
            nc.scalar.activation(column[:], turned[:, :, P - 1], ACT.Copy, scale=0.5)
            half_kb.append(column)

        vw_pool = tile("vw_pool", [P, POOL_PAGES * DV], I32, tag="q_raw0")
        nc.sync.dma_start(
            vw_pool[:].rearrange("p (u e) -> p u e", u=POOL_PAGES),
            v_words.rearrange("u p e b -> p u (e b)").bitcast(I32),
        )
        vsc_pool = tile("vsc_pool", [P, POOL_PAGES * DV], U8, tag="kb_listed")
        nc.gpsimd.memset(vsc_pool[:].bitcast(I32), 0)
        for quad in range(4):
            nc.sync.dma_start(
                vsc_pool[32 * quad : 32 * quad + 4, :].bitcast(I32).rearrange("p (u e) -> p u e", u=POOL_PAGES),
                v_scales[:, 4 * quad : 4 * quad + 4, :].bitcast(I32).rearrange("u f e -> f u e"),
            )

        vs_pool = one_row_pool("vs_pool", vs)

        def key_words(g):
            listed = tile("kw_listed%d" % g, [P, PAGE], U32, tag=["kw_listed0", "q_woven1"][g])
            nc.vector.tensor_copy(listed[:], kw_pool[:].bitcast(U32).indirect(key_list[:, 32 * g : 32 * (g + 1)]))
            dealt = tile("kw_dealt%d" % g, [P, PASSES * PAGE * 2], U8)
            nc.vector.tensor_copy(
                dealt[:].bitcast(U16).rearrange("p (o t c i) -> p o c t i", o=PASSES, t=PACK, i=4),
                listed[:].bitcast(U16).rearrange("p (c i t o) -> p o c t i", o=PASSES, t=PACK, i=4),
            )
            return dealt

        kw_dealt = [key_words(0)]
        for o in range(PASSES):
            codes = tile("q_codes%d" % o, [P, NQ], U32)
            scales = tile("q_scales%d" % o, [P, NQ], U8)
            nc.vector.quantize_mx(out=codes[:].bitcast(FP8X4), scales=scales[:], in_=q_woven[o][:])
            q_codes.append(codes)
            q_scales.append(scales)
        kw_dealt.append(key_words(1))

        inner = [tile("inner%d" % g, [P, PACK, NQ], F32) for g in range(PAGES)]
        outer = {}
        for g in range(PAGES):
            for pair in range(PACK // 2):
                bank = ps.tile([P, 2, NQ], F32, name="scores%d_%d" % (g, pair), tag="scores%d_%d" % (g, pair))
                for u in range(2):
                    t = 2 * pair + u
                    for h in range(HALVES):
                        for o in range(PASSES):
                            kcol = (o * PACK + t) * P
                            scol = o * N + g * PAGE + t * P
                            nc.tensor.matmul_mx(
                                out=bank[:, u, h * P : (h + 1) * P],
                                lhsT=kw_dealt[g][:, 2 * kcol : 2 * (kcol + P)].bitcast(FP4X4),
                                lhsT_scale=k_plane[:, scol : scol + P],
                                rhs=q_codes[o][:, h * P : (h + 1) * P].bitcast(FP8X4),
                                rhs_scale=q_scales[o][:, h * P : (h + 1) * P],
                                start=(o == 0),
                                stop=(o == PASSES - 1),
                            )
                for u in range(2):
                    t = 2 * pair + u
                    nc.scalar.activation(inner[g][:, t, :], bank[:, u, :], ACT.Tanh, bias=half_kb[g][:, t : t + 1], scale=0.5)
            for h in range(HALVES):
                woven = tile("outer%d_%d" % (g, h), [P, P * PACK], F32)
                nc.scalar.activation(
                    woven[:].rearrange("p (c i t) -> p c t i", i=4, t=PACK),
                    inner[g][:, :, h * P : (h + 1) * P].rearrange("p t (c i) -> p c t i", i=4),
                    ACT.Tanh,
                )
                outer[g, h] = woven

        vs_banks = turned_columns("vs", vs_pool, "q_woven1", ["scores0_0", "scores0_1"])
        vsc_listed = tile("vsc_listed", [P, PAGES * DV], U8)
        nc.vector.tensor_copy(vsc_listed[:], vsc_pool[:].indirect(value_list[:]))
        vw_listed = tile("vw_listed", [P, PAGES * DV], U32, tag="kb_listed")
        nc.vector.tensor_copy(vw_listed[:], vw_pool[:].bitcast(U32).indirect(value_list[:]))
        half_vs = tile("half_vs", [P, PAGES * PACK], F32, tag="q_raw0")
        for g in range(PAGES):
            nc.vector.tensor_scalar_mul(half_vs[:, PACK * g : PACK * (g + 1)], vs_banks[g][:, :, P - 1], 0.5)

        w_bf = {}
        for h in range(HALVES):
            for g in range(PAGES):
                w = tile("w%d_%d" % (g, h), [P, P * PACK], BF16)
                nc.vector.scalar_tensor_tensor(
                    out=w[:].rearrange("p (q t) -> p q t", t=PACK),
                    in0=outer[g, h][:].rearrange("p (q t) -> p q t", t=PACK),
                    scalar=1.0,
                    in1=half_vs[:, PACK * g : PACK * (g + 1)].unsqueeze(1).to_broadcast([P, P, PACK]),
                    op0=ALU.add,
                    op1=ALU.mult,
                )
                w_bf[g, h] = w
            acc = ps.tile([P, DV], F32, name="acc%d" % h)
            for g in range(PAGES):
                codes = tile("w_codes%d_%d" % (g, h), [P, P], U32)
                scales = tile("w_scales%d_%d" % (g, h), [P, P], U8)
                nc.vector.quantize_mx(out=codes[:].bitcast(FP8X4), scales=scales[:], in_=w_bf[g, h][:])
                nc.tensor.matmul_mx(
                    out=acc[:],
                    lhsT=codes[:].bitcast(FP8X4),
                    lhsT_scale=scales[:],
                    rhs=vw_listed[:, g * DV : (g + 1) * DV].bitcast(FP8X4),
                    rhs_scale=vsc_listed[:, g * DV : (g + 1) * DV],
                    start=(g == 0),
                    stop=(g == PAGES - 1),
                )
            result = tile("result%d" % h, [P, DV], F32)
            nc.scalar.activation(result[:], acc[:], ACT.Copy, scale=1.0 / 16.0)
            nc.sync.dma_start(out[0, h * P : (h + 1) * P, :], result[:])
